import numpy as np
import ml_dtypes


def mxq(x, axis, fmt="e4m3"):
    dtype, down = {"e4m3": (ml_dtypes.float8_e4m3fn, 7), "e5m2": (ml_dtypes.float8_e5m2, 14)}[fmt]
    v = np.moveaxis(np.asarray(x, np.float32).astype(ml_dtypes.bfloat16).astype(np.float64), axis, -1)
    blocks = v.reshape(v.shape[:-1] + (-1, 32))
    amax = np.abs(blocks).max(-1, keepdims=True)
    byte = np.maximum(np.where(amax > 0, np.frexp(amax)[1] - 1 + 127, 0) - down, 1)
    scale = np.exp2(byte - 127.0)
    codes = (blocks / scale).astype(np.float32).astype(dtype).astype(np.float64)
    return np.moveaxis((codes * scale).reshape(v.shape), -1, axis)


WIDE = False


def mx_kscale(k):
    if not WIDE:
        return np.ones(k)
    levels = np.array([10, -10, 5, -5, 0])
    if k % 512:
        return np.exp2(np.random.permutation(np.resize(levels, k // 32))).repeat(32)
    a = np.empty((k // 512, 16))
    for p in range(k // 512):
        a[p, :8] = np.random.permutation(np.resize(levels, 8))
        for g in range(8):
            far = levels[np.abs(levels - a[p, g]) >= 10]
            a[p, g + 8] = far[np.random.randint(len(far))]
    return np.exp2(a.ravel()).repeat(32)


def f64(x):
    return np.asarray(x).astype(np.float64)


def striped(idx):
    return np.tile(idx.reshape(-1, 16).T, (8, 1)).astype(np.uint16)


def unstriped(offs):
    return offs[:16].T.reshape(-1).astype(np.int64)


def striped8(idx):
    return np.concatenate([x.reshape(-1, 16).T for x in idx]).astype(np.uint16)


def runs(offs, k):
    lists = np.stack([offs[16 * r : 16 * r + 16].T.reshape(-1) for r in range(8)]).astype(np.int64)
    return lists[np.arange(k) % 512 // 64]


def pack_weight(w):
    k, n = w.shape
    w = f64(np.asarray(w, np.float32).astype(ml_dtypes.bfloat16)).reshape(k // 32, 32, n)
    amax = np.abs(w).max(1)
    byte = np.clip(np.where(amax > 0, np.frexp(amax)[1] - 1 + 127 - 7, 1), 1, 254)
    scaled = (w * np.exp2(127.0 - byte)[:, None, :]).reshape(k, n).astype(np.float32)
    words = np.ascontiguousarray(scaled.reshape(k // 512, 128, 4, n).transpose(0, 1, 3, 2)).astype(ml_dtypes.float8_e4m3fn).view(np.uint8)
    return words, np.ascontiguousarray(byte.astype(np.uint8).reshape(k // 512, 16, n))


def unpack_weight(words, scales):
    g, p, n, _ = words.shape
    vals = np.ascontiguousarray(words).view(ml_dtypes.float8_e4m3fn).astype(np.float64) * np.repeat(np.exp2(scales.astype(np.float64) - 127.0), 8, axis=1)[..., None]
    return vals.transpose(0, 1, 3, 2).reshape(g * 512, n)


K, T, S, N, H, W, G = 512, 2048, 256, 512, 512, 128, 1024


def setup_inputs():
    n = np.random.standard_normal
    s = mx_kscale(K)[:, None]
    u = mx_kscale(H)
    packed_xT = pack_weight(n((K, T)) * s)
    perm = np.random.permutation(S)
    return {
        "x_words": packed_xT[0],
        "x_scales": packed_xT[1],
        "w1": (n((K, H)) / np.sqrt(K) / s).astype(np.float32),
        "gn": (np.random.uniform(0.5, 1.5, (H, 1)) * u[:, None]).astype(np.float32),
        "w2": (n((H, N)) / np.sqrt(2 * H) / u[:, None]).astype(np.float32),
        "w3": (n((K, N)) / np.sqrt(2 * K) / s).astype(np.float32),
        "offs": striped(np.random.permutation(T)[:S]),
        "n1": striped(perm[:W]),
        "n2": striped(perm[W:]),
        "hz": striped8(np.random.randint(0, T, (8, S))),
        "n3": striped(np.random.randint(0, S, G)),
    }


def reference(x_words, x_scales, w1, gn, w2, w3, offs, n1, n2, hz, n3):
    xq = unpack_weight(x_words, x_scales)[:, unstriped(offs)]
    y = mxq(f64(w1), 0, "e4m3").T @ xq
    pa = y[:, unstriped(n1)]
    pb = y[:, unstriped(n2)]
    rb = np.minimum(pa, pb)
    ra = np.maximum(pa, pb)
    ds = np.zeros((H, S))
    ds[:, unstriped(n1)] = ra
    dt = ds.copy()
    dt[:, unstriped(n2)] = rb
    z = f64(gn) * dt
    x_hz = unpack_weight(x_words, x_scales)[np.arange(K)[:, None], runs(hz, K)]
    h = mxq(f64(w2), 0, "e4m3").T @ mxq(z, 0, "e4m3") + mxq(f64(w3), 0, "e4m3").T @ x_hz
    ex = np.exp(0.5 * h)
    mb = ex[:, unstriped(n3)]
    ms = mb.reshape(N, S, 4).sum(axis=2)
    return (4.0 * ex) / (ms + 0.5)

@@ -1,0 +1,195 @@
+from contextlib import ExitStack
+
+import concourse.mybir as mybir
+
+K, T, S, N, H, W, G = 512, 2048, 256, 512, 512, 128, 1024
+FLOPS = 2 * S * (K * H + H * N + K * N)
+
+F32 = mybir.dt.float32
+BF16 = mybir.dt.bfloat16
+I32 = mybir.dt.int32
+U32 = mybir.dt.uint32
+U16 = mybir.dt.uint16
+U8 = mybir.dt.uint8
+FP8X4 = mybir.dt.float8_e4m3fn_x4
+ALU = mybir.AluOpType
+ACT = mybir.ActivationFunctionType
+
+P = 128
+PACK = 4
+MEMBERS = 4
+HASH_ROW = 14
+DOWN = 2.0**-62
+UP = 4.0 * DOWN
+
+
+def tile_picked_mixhordergshare_none_p_kernel(tc, x_words, x_scales, w1, gn, w2, w3, offs, n1, n2, hz, n3, out):
+    nc = tc.nc
+    with ExitStack() as ctx:
+        sb = ctx.enter_context(tc.tile_pool(name="sb", bufs=1))
+        ps = ctx.enter_context(tc.psum_pool(name="ps", bufs=1))
+
+        def load_list(name, src):
+            lst = sb.tile(list(src.shape), U16, name=name)
+            nc.sync.dma_start(lst[:], src)
+            return lst
+
+        def load_columns(name, w, cols):
+            raw = sb.tile([P, PACK, cols.stop - cols.start], F32, name=name)
+            nc.sync.dma_start(raw[:], w.rearrange("(p j) c -> p j c", j=PACK)[:, :, cols])
+            return raw
+
+        def load_scale_rows(name, first, zero_engine, queue):
+            table = sb.tile([P, T], U8, name=name)
+            zero_engine.memset(table[:].bitcast(I32), 0)
+            for q in range(4):
+                queue.dma_start(
+                    table[32 * q + first : 32 * q + first + 4, :].bitcast(I32),
+                    x_scales[0, 4 * q : 4 * q + 4, :].bitcast(I32),
+                )
+            return table
+
+        def mx_tiles(name, width):
+            codes = sb.tile([P, width], U32, name=name + "_codes", align_bytes=64)
+            scales = sb.tile([P, width], U8, name=name + "_scales", align_bytes=64)
+            return codes, scales
+
+        def quantize(operand, grouped, cols):
+            codes, scales = operand
+            nc.vector.quantize_mx(
+                out=codes[:, cols].bitcast(FP8X4),
+                scales=scales[:, cols],
+                in_=grouped[:, PACK * cols.start : PACK * cols.stop],
+            )
+
+        def product(acc, weights, cols, tokens, start, stop):
+            nc.tensor.matmul_mx(
+                out=acc[:],
+                lhsT=weights[0][:, cols].bitcast(FP8X4),
+                lhsT_scale=weights[1][:, cols],
+                rhs=tokens[0][:].bitcast(FP8X4),
+                rhs_scale=tokens[1][:],
+                start=start,
+                stop=stop,
+            )
+
+        halves = [slice(0, 256), slice(256, 512)]
+        tiles = [slice(P * t, P * (t + 1)) for t in range(4)]
+
+        offs_sb = load_list("offs_sb", offs)
+        scale_rows = load_scale_rows("scale_rows", 0, nc.vector, nc.scalar)
+        w1_raw = [load_columns("w1_raw%d" % u, w1, halves[u]) for u in range(2)]
+        words = sb.tile([P, T], U32, name="words")
+        nc.sync.dma_start(words[:].bitcast(I32), x_words[0].rearrange("p n t -> p (n t)").bitcast(I32))
+        n1_sb = load_list("n1_sb", n1)
+        n2_sb = load_list("n2_sb", n2)
+        hz_sb = load_list("hz_sb", hz)
+        gain = sb.tile([P, PACK], F32, name="gain")
+        nc.sync.dma_start(gain[:], gn.rearrange("(p t) o -> p (t o)", t=PACK))
+        hashed_rows = load_scale_rows("hashed_rows", HASH_ROW, nc.gpsimd, nc.sync)
+        w3_raw = [load_columns("w3_raw%d" % u, w3, halves[u]) for u in range(2)]
+        w2_raw = [load_columns("w2_raw%d" % u, w2, halves[u]) for u in range(2)]
+        n3_sb = load_list("n3_sb", n3)
+
+        x_pick = mx_tiles("x_pick", S)
+        nc.vector.tensor_copy(x_pick[1][:], scale_rows[:].indirect(offs_sb[:]))
+        w1_bf = sb.tile([P, PACK * H], BF16, name="w1_bf", align_bytes=64)
+        w1_q = mx_tiles("w1_q", H)
+        for u in range(2):
+            nc.vector.tensor_copy(
+                w1_bf[:].rearrange("p (t m j) -> p m j t", t=PACK, j=PACK)[:, 64 * u : 64 * (u + 1)],
+                w1_raw[u][:].rearrange("p j (m t) -> p m j t", t=PACK),
+            )
+        for u in range(2):
+            quantize(w1_q, w1_bf, halves[u])
+        nc.vector.tensor_copy(x_pick[0][:], words[:].indirect(offs_sb[:]))
+
+        work = [sb.tile([P, 3 * S], F32, name="work%d" % t) for t in range(4)]
+        y_sb = [sb.tile([P, S], F32, name="y_sb%d" % t) for t in range(4)]
+        mixed = [sb.tile([P, S], F32, name="mixed%d" % t) for t in range(4)]
+        for t in range(4):
+            y_ps = ps.tile([P, S], F32, name="y_ps%d" % t)
+            product(y_ps, w1_q, tiles[t], x_pick, True, True)
+            nc.vector.tensor_copy(y_sb[t][:], y_ps[:])
+        pa, pb, ra, rb = [[work[t][:, S + W * i : S + W * (i + 1)] for t in range(4)] for i in range(4)]
+        for t in range(4):
+            nc.scalar.activation(pa[t], y_sb[t][:].indirect(n1_sb[:]), ACT.Copy)
+            nc.scalar.activation(pb[t], y_sb[t][:].indirect(n2_sb[:]), ACT.Copy)
+            nc.vector.tensor_tensor(ra[t], pa[t], pb[t], ALU.max)
+            nc.vector.tensor_tensor(rb[t], pa[t], pb[t], ALU.min)
+        for pair in ((0, 1), (2, 3)):
+            for t in pair:
+                nc.scalar.activation(mixed[t][:].indirect(n1_sb[:]), ra[t], ACT.Copy)
+            for t in pair:
+                nc.scalar.activation(mixed[t][:].indirect(n2_sb[:]), rb[t], ACT.Copy)
+
+        hashed_scales = sb.tile([P, S], U8, name="hashed_scales")
+        nc.vector.tensor_copy(hashed_scales[:], hashed_rows[:].indirect(hz_sb[:]))
+        x_hash = mx_tiles("x_hash", S)
+        nc.vector.tensor_copy(x_hash[0][:], words[:].indirect(hz_sb[:]))
+        nc.gpsimd.memset(x_hash[1][:].bitcast(I32), 0)
+        nc.sync.dma_start(x_hash[1][0:100, :].bitcast(I32), hashed_scales[HASH_ROW : HASH_ROW + 100, :].bitcast(I32))
+
+        def prepare(name, raw):
+            grouped = sb.tile([P, PACK * N], BF16, name=name + "_bf", tag=name + "_bf", align_bytes=64)
+            operand = mx_tiles(name + "_q", N)
+            for m in range(4):
+                nc.vector.tensor_copy(
+                    grouped[:, PACK * P * m : PACK * P * (m + 1)].rearrange("p (c i j) -> p c j i", i=4, j=PACK),
+                    raw[m // 2][:, :, P * (m % 2) : P * (m % 2 + 1)].rearrange("p j (c i) -> p c j i", i=4),
+                )
+                quantize(operand, grouped, tiles[m])
+            return operand
+
+        w3_q = prepare("w3", w3_raw)
+        w2_q = prepare("w2", w2_raw)
+
+        z_bf = sb.tile([P, PACK * S], BF16, name="z_bf", tag="w2_bf", align_bytes=64)
+        for t in range(4):
+            nc.vector.tensor_scalar(
+                z_bf[:].rearrange("p (s t) -> p s t", t=PACK)[:, :, t], mixed[t][:], gain[:, t : t + 1], None, ALU.mult
+            )
+        z_q = mx_tiles("z_q", S)
+        quantize(z_q, z_bf, slice(0, S))
+
+        h_ps = [ps.tile([P, S], F32, name="h_ps%d" % m) for m in range(4)]
+        for m in range(4):
+            product(h_ps[m], w3_q, tiles[m], x_hash, True, False)
+        for m in range(4):
+            product(h_ps[m], w2_q, tiles[m], z_q, False, True)
+
+        for m in range(4):
+            ex = work[m]
+            nc.scalar.activation(ex[:, 0:S], h_ps[m][:], ACT.Exp, scale=0.5)
+            members = sb.tile([P, G], F32, name="members%d" % m)
+            den = sb.tile([P, S], F32, name="den%d" % m)
+            inv = sb.tile([P, S], F32, name="inv%d" % m)
+            rec = sb.tile([P, S // 2], F32, name="rec%d" % m)
+            res = sb.tile([P, S], F32, name="res%d" % m)
+            cuts = [0, 128, 256]
+            for a, b in zip(cuts, cuts[1:]):
+                nc.scalar.activation(
+                    members[:, 4 * a : 4 * b],
+                    ex[:].indirect(n3_sb[:, a // 4 : b // 4]),
+                    ACT.Copy,
+                    bias=0.125 * DOWN,
+                    scale=DOWN,
+                )
+            vcuts = [0, 256] if m in (1, 2) else cuts
+            for a, b in zip(vcuts, vcuts[1:]):
+                width = b - a
+                half = width // 2
+                mid = a + half
+                scratch = sb.tile([P, 2 * width + half], F32, name="scratch")
+                four = members[:, 4 * a : 4 * b].rearrange("p (j e) -> p j e", e=4)
+                two = scratch[:, 0 : 2 * width].rearrange("p (j e) -> p j e", e=2)
+                prod = scratch[:, 2 * width :]
+                r = rec[:, a // 2 : b // 2]
+                nc.vector.tensor_tensor(two, four[:, :, 0:2], four[:, :, 2:4], ALU.add)
+                nc.vector.tensor_tensor(den[:, a:b], two[:, :, 0], two[:, :, 1], ALU.add)
+                nc.vector.tensor_tensor(prod, den[:, a:mid], den[:, mid:b], ALU.mult)
+                nc.vector.reciprocal(r, prod)
+                nc.vector.tensor_tensor(inv[:, a:mid], den[:, mid:b], r, ALU.mult)
+                nc.vector.tensor_tensor(inv[:, mid:b], den[:, a:mid], r, ALU.mult)
+                nc.vector.scalar_tensor_tensor(res[:, a:b], inv[:, a:b], UP, ex[:, a:b], ALU.mult, ALU.mult)
+                nc.sync.dma_start(out[tiles[m], a:b], res[:, a:b])

@@ -19,8 +19,8 @@ P = 128
 PACK = 4
 MEMBERS = 4
 HASH_ROW = 14
-DOWN = 2.0**-62
-UP = 4.0 * DOWN
+DOWN = 2.0**-122
+UP = 2.0**120
 
 
 def tile_picked_mixhordergshare_none_p_kernel(tc, x_words, x_scales, w1, gn, w2, w3, offs, n1, n2, hz, n3, out):
@@ -40,7 +40,7 @@ def tile_picked_mixhordergshare_none_p_kernel(tc, x_words, x_scales, w1, gn, w2,
             return raw
 
         def load_scale_rows(name, first, zero_engine, queue):
-            table = sb.tile([P, T], U8, name=name)
+            table = sb.tile([P, T], U8, name=name, align_bytes=64)
             zero_engine.memset(table[:].bitcast(I32), 0)
             for q in range(4):
                 queue.dma_start(
@@ -62,13 +62,13 @@ def tile_picked_mixhordergshare_none_p_kernel(tc, x_words, x_scales, w1, gn, w2,
                 in_=grouped[:, PACK * cols.start : PACK * cols.stop],
             )
 
-        def product(acc, weights, cols, tokens, start, stop):
+        def product(acc, weights, cols, tokens, start, stop, places=slice(0, S)):
             nc.tensor.matmul_mx(
-                out=acc[:],
+                out=acc[:, places],
                 lhsT=weights[0][:, cols].bitcast(FP8X4),
                 lhsT_scale=weights[1][:, cols],
-                rhs=tokens[0][:].bitcast(FP8X4),
-                rhs_scale=tokens[1][:],
+                rhs=tokens[0][:, places].bitcast(FP8X4),
+                rhs_scale=tokens[1][:, places],
                 start=start,
                 stop=stop,
             )
@@ -77,18 +77,18 @@ def tile_picked_mixhordergshare_none_p_kernel(tc, x_words, x_scales, w1, gn, w2,
         tiles = [slice(P * t, P * (t + 1)) for t in range(4)]
 
         offs_sb = load_list("offs_sb", offs)
+        n1_sb = load_list("n1_sb", n1)
+        n2_sb = load_list("n2_sb", n2)
+        hz_sb = load_list("hz_sb", hz)
         scale_rows = load_scale_rows("scale_rows", 0, nc.vector, nc.scalar)
         w1_raw = [load_columns("w1_raw%d" % u, w1, halves[u]) for u in range(2)]
         words = sb.tile([P, T], U32, name="words")
         nc.sync.dma_start(words[:].bitcast(I32), x_words[0].rearrange("p n t -> p (n t)").bitcast(I32))
-        n1_sb = load_list("n1_sb", n1)
-        n2_sb = load_list("n2_sb", n2)
-        hz_sb = load_list("hz_sb", hz)
         gain = sb.tile([P, PACK], F32, name="gain")
         nc.sync.dma_start(gain[:], gn.rearrange("(p t) o -> p (t o)", t=PACK))
-        hashed_rows = load_scale_rows("hashed_rows", HASH_ROW, nc.gpsimd, nc.sync)
-        w3_raw = [load_columns("w3_raw%d" % u, w3, halves[u]) for u in range(2)]
-        w2_raw = [load_columns("w2_raw%d" % u, w2, halves[u]) for u in range(2)]
+        w3_raw = load_columns("w3_raw", w3, slice(0, N))
+        hashed_rows = load_scale_rows("staging", HASH_ROW, nc.gpsimd, nc.sync)
+        w2_raw = load_columns("w2_raw", w2, slice(0, N))
         n3_sb = load_list("n3_sb", n3)
 
         x_pick = mx_tiles("x_pick", S)
@@ -130,66 +130,86 @@ def tile_picked_mixhordergshare_none_p_kernel(tc, x_words, x_scales, w1, gn, w2,
         nc.gpsimd.memset(x_hash[1][:].bitcast(I32), 0)
         nc.sync.dma_start(x_hash[1][0:100, :].bitcast(I32), hashed_scales[HASH_ROW : HASH_ROW + 100, :].bitcast(I32))
 
-        def prepare(name, raw):
-            grouped = sb.tile([P, PACK * N], BF16, name=name + "_bf", tag=name + "_bf", align_bytes=64)
+        def prepare(name, raw, tag):
+            grouped = sb.tile([P, PACK * N], BF16, name=name + "_bf", tag=tag, align_bytes=64)
             operand = mx_tiles(name + "_q", N)
             for m in range(4):
                 nc.vector.tensor_copy(
                     grouped[:, PACK * P * m : PACK * P * (m + 1)].rearrange("p (c i j) -> p c j i", i=4, j=PACK),
-                    raw[m // 2][:, :, P * (m % 2) : P * (m % 2 + 1)].rearrange("p j (c i) -> p c j i", i=4),
+                    raw[:, :, tiles[m]].rearrange("p j (c i) -> p c j i", i=4),
                 )
                 quantize(operand, grouped, tiles[m])
             return operand
 
-        w3_q = prepare("w3", w3_raw)
-        w2_q = prepare("w2", w2_raw)
+        w3_q = prepare("w3", w3_raw, "w3_bf")
+        w2_q = prepare("w2", w2_raw, "staging")
 
-        z_bf = sb.tile([P, PACK * S], BF16, name="z_bf", tag="w2_bf", align_bytes=64)
-        for t in range(4):
-            nc.vector.tensor_scalar(
-                z_bf[:].rearrange("p (s t) -> p s t", t=PACK)[:, :, t], mixed[t][:], gain[:, t : t + 1], None, ALU.mult
-            )
+        z_bf = sb.tile([P, PACK * S], BF16, name="z_bf", tag="staging", align_bytes=64)
+        z_view = z_bf[:].rearrange("p (s t) -> p s t", t=PACK)
         z_q = mx_tiles("z_q", S)
-        quantize(z_q, z_bf, slice(0, S))
+        for t in range(3):
+            nc.vector.tensor_scalar(z_view[:, :, t], mixed[t][:], gain[:, t : t + 1], None, ALU.mult)
+        for cols in tiles[:2]:
+            nc.vector.tensor_scalar(z_view[:, cols, 3], mixed[3][:, cols], gain[:, 3:4], None, ALU.mult)
+        for cols in tiles[:2]:
+            quantize(z_q, z_bf, cols)
 
         h_ps = [ps.tile([P, S], F32, name="h_ps%d" % m) for m in range(4)]
         for m in range(4):
             product(h_ps[m], w3_q, tiles[m], x_hash, True, False)
-        for m in range(4):
+        product(h_ps[0], w2_q, tiles[0], z_q, False, False, tiles[0])
+        product(h_ps[0], w2_q, tiles[0], z_q, False, True, tiles[1])
+        for m in range(1, 4):
             product(h_ps[m], w2_q, tiles[m], z_q, False, True)
 
-        for m in range(4):
-            ex = work[m]
-            nc.scalar.activation(ex[:, 0:S], h_ps[m][:], ACT.Exp, scale=0.5)
-            members = sb.tile([P, G], F32, name="members%d" % m)
-            den = sb.tile([P, S], F32, name="den%d" % m)
-            inv = sb.tile([P, S], F32, name="inv%d" % m)
-            rec = sb.tile([P, S // 2], F32, name="rec%d" % m)
-            res = sb.tile([P, S], F32, name="res%d" % m)
-            cuts = [0, 128, 256]
-            for a, b in zip(cuts, cuts[1:]):
-                nc.scalar.activation(
-                    members[:, 4 * a : 4 * b],
-                    ex[:].indirect(n3_sb[:, a // 4 : b // 4]),
-                    ACT.Copy,
-                    bias=0.125 * DOWN,
-                    scale=DOWN,
-                )
-            vcuts = [0, 256] if m in (1, 2) else cuts
-            for a, b in zip(vcuts, vcuts[1:]):
-                width = b - a
-                half = width // 2
-                mid = a + half
-                scratch = sb.tile([P, 2 * width + half], F32, name="scratch")
-                four = members[:, 4 * a : 4 * b].rearrange("p (j e) -> p j e", e=4)
-                two = scratch[:, 0 : 2 * width].rearrange("p (j e) -> p j e", e=2)
-                prod = scratch[:, 2 * width :]
-                r = rec[:, a // 2 : b // 2]
-                nc.vector.tensor_tensor(two, four[:, :, 0:2], four[:, :, 2:4], ALU.add)
-                nc.vector.tensor_tensor(den[:, a:b], two[:, :, 0], two[:, :, 1], ALU.add)
-                nc.vector.tensor_tensor(prod, den[:, a:mid], den[:, mid:b], ALU.mult)
-                nc.vector.reciprocal(r, prod)
-                nc.vector.tensor_tensor(inv[:, a:mid], den[:, mid:b], r, ALU.mult)
-                nc.vector.tensor_tensor(inv[:, mid:b], den[:, a:mid], r, ALU.mult)
-                nc.vector.scalar_tensor_tensor(res[:, a:b], inv[:, a:b], UP, ex[:, a:b], ALU.mult, ALU.mult)
-                nc.sync.dma_start(out[tiles[m], a:b], res[:, a:b])
+        cuts = [(0, 64, 128, 256), (0, 128, 256), (0, 128, 256), (0, 128, 192, 256)]
+        chunks = [(m, a, b) for m in range(4) for a, b in zip(cuts[m], cuts[m][1:])]
+        res = [sb.tile([P, S], F32, name="res%d" % m) for m in range(4)]
+
+        def look_up(m, a, b, scale):
+            if a == 0:
+                nc.scalar.activation(work[m][:, 0:S], h_ps[m][:], ACT.Exp, scale=0.5)
+            members = sb.tile([P, MEMBERS * (b - a)], F32, name="members", bufs=4)
+            nc.scalar.activation(
+                members[:], work[m][:].indirect(n3_sb[:, a // 4 : b // 4]), ACT.Copy, bias=0.125 * scale, scale=scale
+            )
+            den = sb.tile([P, b - a], F32, name="den", bufs=3)
+            nc.vector.tensor_reduce(den[:], members[:].rearrange("p (j e) -> p j e", e=MEMBERS), mybir.AxisListType.X, ALU.add)
+            return den
+
+        def pair_up(den):
+            half = den.shape[1] // 2
+            prod = sb.tile([P, half], F32, name="prod", bufs=3)
+            nc.vector.scalar_tensor_tensor(prod[:], den[:, :half], UP, den[:, half:], ALU.mult, ALU.mult)
+            return prod
+
+        def divide(m, a, b, den, prod):
+            half = (b - a) // 2
+            rec = sb.tile([P, half], F32, name="rec", bufs=3)
+            nc.vector.reciprocal(rec[:], prod[:])
+            inv = sb.tile([P, 2, half], F32, name="inv", bufs=3)
+            nc.gpsimd.tensor_tensor(
+                inv[:],
+                den[:].rearrange("p (u h) -> p u h", u=2)[:, ::-1, :],
+                rec[:].unsqueeze(1).to_broadcast([P, 2, half]),
+                ALU.mult,
+            )
+            nc.gpsimd.tensor_tensor(res[m][:, a:b], inv[:].rearrange("p u h -> p (u h)"), work[m][:, a:b], ALU.mult)
+            if m == 3:
+                nc.sync.dma_start(out[tiles[m], a:b], res[m][:, a:b])
+            elif b == S:
+                nc.sync.dma_start(out[tiles[m], :], res[m][:])
+
+        den = look_up(*chunks[0], DOWN)
+        prod = pair_up(den)
+        for c in range(1, len(chunks) - 1):
+            next_den = look_up(*chunks[c], DOWN)
+            divide(*chunks[c - 1], den, prod)
+            den, prod = next_den, pair_up(next_den)
+        m, a, b = chunks[-1]
+        last_den = look_up(m, a, b, 0.25)
+        divide(*chunks[-2], den, prod)
+        last_inv = sb.tile([P, b - a], F32, name="last_inv")
+        nc.vector.reciprocal(last_inv[:], last_den[:])
+        nc.vector.tensor_tensor(res[m][:, a:b], last_inv[:], work[m][:, a:b], ALU.mult)
+        nc.sync.dma_start(out[tiles[m], a:b], res[m][:, a:b])

@@ -162,13 +162,16 @@ def tile_picked_mixhordergshare_none_p_kernel(tc, x_words, x_scales, w1, gn, w2,
         for m in range(1, 4):
             product(h_ps[m], w2_q, tiles[m], z_q, False, True)
 
-        cuts = [(0, 64, 128, 256), (0, 128, 256), (0, 128, 256), (0, 128, 192, 256)]
+        cuts = [(0, 128, 256)] * 4
         chunks = [(m, a, b) for m in range(4) for a, b in zip(cuts[m], cuts[m][1:])]
         res = [sb.tile([P, S], F32, name="res%d" % m) for m in range(4)]
 
+        def exponential(m):
+            nc.scalar.activation(work[m][:, 0:S], h_ps[m][:], ACT.Exp, scale=0.5)
+
         def look_up(m, a, b, scale):
-            if a == 0:
-                nc.scalar.activation(work[m][:, 0:S], h_ps[m][:], ACT.Exp, scale=0.5)
+            if b == S and m < 3:
+                exponential(m + 1)
             members = sb.tile([P, MEMBERS * (b - a)], F32, name="members", bufs=4)
             nc.scalar.activation(
                 members[:], work[m][:].indirect(n3_sb[:, a // 4 : b // 4]), ACT.Copy, bias=0.125 * scale, scale=scale
@@ -183,33 +186,34 @@ def tile_picked_mixhordergshare_none_p_kernel(tc, x_words, x_scales, w1, gn, w2,
             nc.vector.scalar_tensor_tensor(prod[:], den[:, :half], UP, den[:, half:], ALU.mult, ALU.mult)
             return prod
 
-        def divide(m, a, b, den, prod):
+        def divide(m, a, b, den, prod, engine):
             half = (b - a) // 2
             rec = sb.tile([P, half], F32, name="rec", bufs=3)
             nc.vector.reciprocal(rec[:], prod[:])
             inv = sb.tile([P, 2, half], F32, name="inv", bufs=3)
-            nc.gpsimd.tensor_tensor(
+            engine.tensor_tensor(
                 inv[:],
                 den[:].rearrange("p (u h) -> p u h", u=2)[:, ::-1, :],
                 rec[:].unsqueeze(1).to_broadcast([P, 2, half]),
                 ALU.mult,
             )
-            nc.gpsimd.tensor_tensor(res[m][:, a:b], inv[:].rearrange("p u h -> p (u h)"), work[m][:, a:b], ALU.mult)
+            engine.tensor_tensor(res[m][:, a:b], inv[:].rearrange("p u h -> p (u h)"), work[m][:, a:b], ALU.mult)
             if m == 3:
                 nc.sync.dma_start(out[tiles[m], a:b], res[m][:, a:b])
             elif b == S:
                 nc.sync.dma_start(out[tiles[m], :], res[m][:])
 
+        exponential(0)
         den = look_up(*chunks[0], DOWN)
         prod = pair_up(den)
         for c in range(1, len(chunks) - 1):
             next_den = look_up(*chunks[c], DOWN)
-            divide(*chunks[c - 1], den, prod)
+            divide(*chunks[c - 1], den, prod, nc.gpsimd)
             den, prod = next_den, pair_up(next_den)
         m, a, b = chunks[-1]
         last_den = look_up(m, a, b, 0.25)
-        divide(*chunks[-2], den, prod)
+        divide(*chunks[-2], den, prod, nc.gpsimd)
         last_inv = sb.tile([P, b - a], F32, name="last_inv")
         nc.vector.reciprocal(last_inv[:], last_den[:])
         nc.vector.tensor_tensor(res[m][:, a:b], last_inv[:], work[m][:, a:b], ALU.mult)
-        nc.sync.dma_start(out[tiles[m], a:b], res[m][:, a:b])
+        nc.scalar.dma_start(out[tiles[m], a:b], res[m][:, a:b])

from contextlib import ExitStack

import concourse.mybir as mybir

K, T, S, N, H, W, G = 512, 2048, 256, 512, 512, 128, 1024
FLOPS = 2 * S * (K * H + H * N + K * N)

F32 = mybir.dt.float32
BF16 = mybir.dt.bfloat16
I32 = mybir.dt.int32
U32 = mybir.dt.uint32
U16 = mybir.dt.uint16
U8 = mybir.dt.uint8
FP8X4 = mybir.dt.float8_e4m3fn_x4
ALU = mybir.AluOpType
ACT = mybir.ActivationFunctionType

P = 128
PACK = 4
MEMBERS = 4
HASH_ROW = 14
DOWN = 2.0**-122
UP = 2.0**120


def tile_picked_mixhordergshare_none_p_kernel(tc, x_words, x_scales, w1, gn, w2, w3, offs, n1, n2, hz, n3, out):
    nc = tc.nc
    with ExitStack() as ctx:
        sb = ctx.enter_context(tc.tile_pool(name="sb", bufs=1))
        ps = ctx.enter_context(tc.psum_pool(name="ps", bufs=1))

        def load_list(name, src):
            lst = sb.tile(list(src.shape), U16, name=name)
            nc.sync.dma_start(lst[:], src)
            return lst

        def load_columns(name, w, cols):
            raw = sb.tile([P, PACK, cols.stop - cols.start], F32, name=name)
            nc.sync.dma_start(raw[:], w.rearrange("(p j) c -> p j c", j=PACK)[:, :, cols])
            return raw

        def load_scale_rows(name, first, zero_engine, queue):
            table = sb.tile([P, T], U8, name=name, align_bytes=64)
            zero_engine.memset(table[:].bitcast(I32), 0)
            for q in range(4):
                queue.dma_start(
                    table[32 * q + first : 32 * q + first + 4, :].bitcast(I32),
                    x_scales[0, 4 * q : 4 * q + 4, :].bitcast(I32),
                )
            return table

        def mx_tiles(name, width):
            codes = sb.tile([P, width], U32, name=name + "_codes", align_bytes=64)
            scales = sb.tile([P, width], U8, name=name + "_scales", align_bytes=64)
            return codes, scales

        def quantize(operand, grouped, cols):
            codes, scales = operand
            nc.vector.quantize_mx(
                out=codes[:, cols].bitcast(FP8X4),
                scales=scales[:, cols],
                in_=grouped[:, PACK * cols.start : PACK * cols.stop],
            )

        def product(acc, weights, cols, tokens, start, stop, places=slice(0, S)):
            nc.tensor.matmul_mx(
                out=acc[:, places],
                lhsT=weights[0][:, cols].bitcast(FP8X4),
                lhsT_scale=weights[1][:, cols],
                rhs=tokens[0][:, places].bitcast(FP8X4),
                rhs_scale=tokens[1][:, places],
                start=start,
                stop=stop,
            )

        halves = [slice(0, 256), slice(256, 512)]
        tiles = [slice(P * t, P * (t + 1)) for t in range(4)]

        offs_sb = load_list("offs_sb", offs)
        n1_sb = load_list("n1_sb", n1)
        n2_sb = load_list("n2_sb", n2)
        hz_sb = load_list("hz_sb", hz)
        scale_rows = load_scale_rows("scale_rows", 0, nc.vector, nc.scalar)
        w1_raw = [load_columns("w1_raw%d" % u, w1, halves[u]) for u in range(2)]
        words = sb.tile([P, T], U32, name="words")
        nc.sync.dma_start(words[:].bitcast(I32), x_words[0].rearrange("p n t -> p (n t)").bitcast(I32))
        gain = sb.tile([P, PACK], F32, name="gain")
        nc.sync.dma_start(gain[:], gn.rearrange("(p t) o -> p (t o)", t=PACK))
        w3_raw = load_columns("w3_raw", w3, slice(0, N))
        hashed_rows = load_scale_rows("staging", HASH_ROW, nc.gpsimd, nc.sync)
        w2_raw = load_columns("w2_raw", w2, slice(0, N))
        n3_sb = load_list("n3_sb", n3)

        x_pick = mx_tiles("x_pick", S)
        nc.vector.tensor_copy(x_pick[1][:], scale_rows[:].indirect(offs_sb[:]))
        w1_bf = sb.tile([P, PACK * H], BF16, name="w1_bf", align_bytes=64)
        w1_q = mx_tiles("w1_q", H)
        for u in range(2):
            nc.vector.tensor_copy(
                w1_bf[:].rearrange("p (t m j) -> p m j t", t=PACK, j=PACK)[:, 64 * u : 64 * (u + 1)],
                w1_raw[u][:].rearrange("p j (m t) -> p m j t", t=PACK),
            )
        for u in range(2):
            quantize(w1_q, w1_bf, halves[u])
        nc.vector.tensor_copy(x_pick[0][:], words[:].indirect(offs_sb[:]))

        work = [sb.tile([P, 3 * S], F32, name="work%d" % t) for t in range(4)]
        y_sb = [sb.tile([P, S], F32, name="y_sb%d" % t) for t in range(4)]
        mixed = [sb.tile([P, S], F32, name="mixed%d" % t) for t in range(4)]
        for t in range(4):
            y_ps = ps.tile([P, S], F32, name="y_ps%d" % t)
            product(y_ps, w1_q, tiles[t], x_pick, True, True)
            nc.vector.tensor_copy(y_sb[t][:], y_ps[:])
        pa, pb, ra, rb = [[work[t][:, S + W * i : S + W * (i + 1)] for t in range(4)] for i in range(4)]
        for t in range(4):
            nc.scalar.activation(pa[t], y_sb[t][:].indirect(n1_sb[:]), ACT.Copy)
            nc.scalar.activation(pb[t], y_sb[t][:].indirect(n2_sb[:]), ACT.Copy)
            nc.vector.tensor_tensor(ra[t], pa[t], pb[t], ALU.max)
            nc.vector.tensor_tensor(rb[t], pa[t], pb[t], ALU.min)
        for pair in ((0, 1), (2, 3)):
            for t in pair:
                nc.scalar.activation(mixed[t][:].indirect(n1_sb[:]), ra[t], ACT.Copy)
            for t in pair:
                nc.scalar.activation(mixed[t][:].indirect(n2_sb[:]), rb[t], ACT.Copy)

        hashed_scales = sb.tile([P, S], U8, name="hashed_scales")
        nc.vector.tensor_copy(hashed_scales[:], hashed_rows[:].indirect(hz_sb[:]))
        x_hash = mx_tiles("x_hash", S)
        nc.vector.tensor_copy(x_hash[0][:], words[:].indirect(hz_sb[:]))
        nc.gpsimd.memset(x_hash[1][:].bitcast(I32), 0)
        nc.sync.dma_start(x_hash[1][0:100, :].bitcast(I32), hashed_scales[HASH_ROW : HASH_ROW + 100, :].bitcast(I32))

        def prepare(name, raw, tag):
            grouped = sb.tile([P, PACK * N], BF16, name=name + "_bf", tag=tag, align_bytes=64)
            operand = mx_tiles(name + "_q", N)
            for m in range(4):
                nc.vector.tensor_copy(
                    grouped[:, PACK * P * m : PACK * P * (m + 1)].rearrange("p (c i j) -> p c j i", i=4, j=PACK),
                    raw[:, :, tiles[m]].rearrange("p j (c i) -> p c j i", i=4),
                )
                quantize(operand, grouped, tiles[m])
            return operand

        w3_q = prepare("w3", w3_raw, "w3_bf")
        w2_q = prepare("w2", w2_raw, "staging")

        z_bf = sb.tile([P, PACK * S], BF16, name="z_bf", tag="staging", align_bytes=64)
        z_view = z_bf[:].rearrange("p (s t) -> p s t", t=PACK)
        z_q = mx_tiles("z_q", S)
        for t in range(3):
            nc.vector.tensor_scalar(z_view[:, :, t], mixed[t][:], gain[:, t : t + 1], None, ALU.mult)
        for cols in tiles[:2]:
            nc.vector.tensor_scalar(z_view[:, cols, 3], mixed[3][:, cols], gain[:, 3:4], None, ALU.mult)
        for cols in tiles[:2]:
            quantize(z_q, z_bf, cols)

        h_ps = [ps.tile([P, S], F32, name="h_ps%d" % m) for m in range(4)]
        for m in range(4):
            product(h_ps[m], w3_q, tiles[m], x_hash, True, False)
        product(h_ps[0], w2_q, tiles[0], z_q, False, False, tiles[0])
        product(h_ps[0], w2_q, tiles[0], z_q, False, True, tiles[1])
        for m in range(1, 4):
            product(h_ps[m], w2_q, tiles[m], z_q, False, True)

        cuts = [(0, 128, 256)] * 4
        chunks = [(m, a, b) for m in range(4) for a, b in zip(cuts[m], cuts[m][1:])]
        res = [sb.tile([P, S], F32, name="res%d" % m) for m in range(4)]

        def exponential(m):
            nc.scalar.activation(work[m][:, 0:S], h_ps[m][:], ACT.Exp, scale=0.5)

        def look_up(m, a, b, scale):
            if b == S and m < 3:
                exponential(m + 1)
            members = sb.tile([P, MEMBERS * (b - a)], F32, name="members", bufs=4)
            nc.scalar.activation(
                members[:], work[m][:].indirect(n3_sb[:, a // 4 : b // 4]), ACT.Copy, bias=0.125 * scale, scale=scale
            )
            den = sb.tile([P, b - a], F32, name="den", bufs=3)
            nc.vector.tensor_reduce(den[:], members[:].rearrange("p (j e) -> p j e", e=MEMBERS), mybir.AxisListType.X, ALU.add)
            return den

        def pair_up(den):
            half = den.shape[1] // 2
            prod = sb.tile([P, half], F32, name="prod", bufs=3)
            nc.vector.scalar_tensor_tensor(prod[:], den[:, :half], UP, den[:, half:], ALU.mult, ALU.mult)
            return prod

        def divide(m, a, b, den, prod, engine):
            half = (b - a) // 2
            rec = sb.tile([P, half], F32, name="rec", bufs=3)
            nc.vector.reciprocal(rec[:], prod[:])
            inv = sb.tile([P, 2, half], F32, name="inv", bufs=3)
            engine.tensor_tensor(
                inv[:],
                den[:].rearrange("p (u h) -> p u h", u=2)[:, ::-1, :],
                rec[:].unsqueeze(1).to_broadcast([P, 2, half]),
                ALU.mult,
            )
            engine.tensor_tensor(res[m][:, a:b], inv[:].rearrange("p u h -> p (u h)"), work[m][:, a:b], ALU.mult)
            if m == 3:
                nc.sync.dma_start(out[tiles[m], a:b], res[m][:, a:b])
            elif b == S:
                nc.sync.dma_start(out[tiles[m], :], res[m][:])

        exponential(0)
        den = look_up(*chunks[0], DOWN)
        prod = pair_up(den)
        for c in range(1, len(chunks) - 1):
            next_den = look_up(*chunks[c], DOWN)
            divide(*chunks[c - 1], den, prod, nc.gpsimd)
            den, prod = next_den, pair_up(next_den)
        m, a, b = chunks[-1]
        last_den = look_up(m, a, b, 0.25)
        divide(*chunks[-2], den, prod, nc.gpsimd)
        last_inv = sb.tile([P, b - a], F32, name="last_inv")
        nc.vector.reciprocal(last_inv[:], last_den[:])
        nc.vector.tensor_tensor(res[m][:, a:b], last_inv[:], work[m][:, a:b], ALU.mult)
        nc.scalar.dma_start(out[tiles[m], a:b], res[m][:, a:b])
